import numpy as np
import ml_dtypes


def mxq(x, axis, fmt="e4m3"):
    dtype, down = {"e4m3": (ml_dtypes.float8_e4m3fn, 7), "e5m2": (ml_dtypes.float8_e5m2, 14)}[fmt]
    v = np.moveaxis(np.asarray(x, np.float32).astype(ml_dtypes.bfloat16).astype(np.float64), axis, -1)
    blocks = v.reshape(v.shape[:-1] + (-1, 32))
    amax = np.abs(blocks).max(-1, keepdims=True)
    byte = np.maximum(np.where(amax > 0, np.frexp(amax)[1] - 1 + 127, 0) - down, 1)
    scale = np.exp2(byte - 127.0)
    codes = (blocks / scale).astype(np.float32).astype(dtype).astype(np.float64)
    return np.moveaxis((codes * scale).reshape(v.shape), -1, axis)


WIDE = False


def mx_kscale(k):
    if not WIDE:
        return np.ones(k)
    levels = np.array([10, -10, 5, -5, 0])
    if k % 512:
        return np.exp2(np.random.permutation(np.resize(levels, k // 32))).repeat(32)
    a = np.empty((k // 512, 16))
    for p in range(k // 512):
        a[p, :8] = np.random.permutation(np.resize(levels, 8))
        for g in range(8):
            far = levels[np.abs(levels - a[p, g]) >= 10]
            a[p, g + 8] = far[np.random.randint(len(far))]
    return np.exp2(a.ravel()).repeat(32)


def f64(x):
    return np.asarray(x).astype(np.float64)


def striped(idx):
    return np.tile(np.asarray(idx).reshape(-1, 16).T, (8, 1)).astype(np.uint16)


def unstriped(offs):
    return offs[:16].T.reshape(-1).astype(np.int64)


E2M1 = np.array([0.0, 0.5, 1.0, 1.5, 2.0, 3.0, 4.0, 6.0, -0.0, -0.5, -1.0, -1.5, -2.0, -3.0, -4.0, -6.0])


def pack_weight(w, fmt):
    k, n = w.shape
    w = f64(np.asarray(w, np.float32).astype(ml_dtypes.bfloat16)).reshape(k // 32, 32, n)
    amax = np.abs(w).max(1)
    if fmt == "e4m3":
        byte = np.frexp(amax)[1] - 1 + 127 - 7
    else:
        mant, ex = np.frexp(amax / 6.0)
        byte = np.where(mant > 0.5, ex, ex - 1) + 127
    byte = np.clip(np.where(amax > 0, byte, 1), 1, 254)
    scaled = (w * np.exp2(127.0 - byte)[:, None, :]).reshape(k, n).astype(np.float32)
    by_word = np.ascontiguousarray(scaled.reshape(k // 512, 128, 4, n).transpose(0, 1, 3, 2))
    if fmt == "e4m3":
        words = by_word.astype(ml_dtypes.float8_e4m3fn).view(np.uint8)
    else:
        c = by_word.astype(ml_dtypes.float4_e2m1fn).view(np.uint8) & 0xF
        words = (c[..., 0::2] | (c[..., 1::2] << 4)).reshape(k // 512, 128, 2 * n)
    return np.ascontiguousarray(words), np.ascontiguousarray(byte.astype(np.uint8).reshape(k // 512, 16, n))


def unpack_weight(words, scales, fmt):
    g, _, n = scales.shape
    words = np.ascontiguousarray(words).reshape(g, 128, n, -1)
    if fmt == "e4m3":
        vals = words.view(ml_dtypes.float8_e4m3fn).astype(np.float64)
    else:
        nib = np.empty((g, 128, n, 4), np.uint8)
        nib[..., 0::2] = words & 0xF
        nib[..., 1::2] = words >> 4
        vals = E2M1[nib]
    vals = vals * np.repeat(np.exp2(scales.astype(np.float64) - 127.0), 8, axis=1)[..., None]
    return vals.transpose(0, 1, 3, 2).reshape(g * 512, n)


D, T, I, Q, E, U = 512, 1024, 512, 128, 512, 256


def setup_inputs():
    n = np.random.standard_normal
    idx = np.random.permutation(T)[:I]
    idx2 = np.random.randint(0, U, I)
    fd = mx_kscale(D)
    fi = mx_kscale(I)
    keysp = pack_weight(n((D, T)) / fd[:, None], "e4m3")
    return {
        "query": (n((D, Q)) * 0.25 / np.sqrt(D) * fd[:, None]).astype(np.float32),
        "keys_words": keysp[0],
        "keys_scales": keysp[1],
        "size": (np.random.uniform(0.5, 2.0, (1, I)) * fi).astype(np.float32),
        "vals": (n((E, T))).astype(np.float32),
        "low": (np.random.uniform(-1.5, -0.3, (E, U))).astype(np.float32),
        "high": (np.random.uniform(0.3, 1.5, (E, U))).astype(np.float32),
        "vsc": (np.random.uniform(0.5, 2.0, (I, 1)) / fi[:, None]).astype(np.float32),
        "offs": striped(idx),
        "offs2": striped(idx2),
    }


def reference(query, keys_words, keys_scales, size, vals, low, high, vsc, offs, offs2):
    idx = unstriped(offs)
    idx2 = unstriped(offs2)
    keysu = unpack_weight(keys_words, keys_scales, "e4m3")
    queryq = mxq(f64(query), 0, "e4m3")
    keysidxg = keysu[:, idx]
    a = queryq.T @ keysidxg
    p = np.exp(a - np.max(a, axis=1, keepdims=True))
    w = p * f64(size) / np.sum(p, axis=1, keepdims=True)
    wt = w.T
    vb = np.minimum(np.maximum(f64(vals)[:, idx], f64(low)[:, idx2]), f64(high)[:, idx2])
    vt = vb.T
    vv = vt * f64(vsc)
    wtq = mxq(wt, 0, "e4m3")
    vvq = mxq(vv, 0, "e4m3")
    o = wtq.T @ vvq
    return o

@@ -1,0 +1,204 @@
+from contextlib import ExitStack
+
+import concourse.mybir as mybir
+from concourse.masks import make_identity
+
+F32 = mybir.dt.float32
+BF16 = mybir.dt.bfloat16
+I32 = mybir.dt.int32
+U32 = mybir.dt.uint32
+U16 = mybir.dt.uint16
+U8 = mybir.dt.uint8
+FP8X4 = mybir.dt.float8_e4m3fn_x4
+ALU = mybir.AluOpType
+ACT = mybir.ActivationFunctionType
+
+P = 128
+D, T, I, Q, E, U = 512, 1024, 512, 128, 512, 256
+FLOPS = 2 * D * Q * I + 2 * I * Q * E
+BLOCKS = E // P
+BOUND_W = I + 8
+VALS_ON_VECTOR = (512, 0, 512, 0)
+
+
+def tile_attend_boundedvalues_kernel(tc, query, keys_words, keys_scales, size, vals, low, high, vsc, offs, offs2, out):
+    nc = tc.nc
+    with ExitStack() as ctx:
+        sb = ctx.enter_context(tc.tile_pool(name="sb", bufs=1))
+        ps = ctx.enter_context(tc.psum_pool(name="ps", bufs=1))
+        ps_turn = ctx.enter_context(tc.psum_pool(name="ps_turn", bufs=3))
+
+        def dealt(ap):
+            return ap.rearrange("p (t b r) -> p b t r", t=4, r=8)
+
+        def natural(ap):
+            return ap.rearrange("p (b t r) -> p b t r", t=4, r=8)
+
+        tok_list = sb.tile([P, I // 16], U16, name="tok_list")
+        cls_list = sb.tile([P, I // 16], U16, name="cls_list")
+        lo_win = [sb.tile([P, BOUND_W], F32, name=f"lo_win{j}") for j in range(BLOCKS)]
+        hi_win = [sb.tile([P, BOUND_W], F32, name=f"hi_win{j}") for j in range(BLOCKS)]
+        val_win = [sb.tile([P, T], F32, name=f"val_win{j}") for j in range(BLOCKS)]
+        q_raw = sb.tile([P, 4, Q], F32, name="q_raw")
+        kw_win = sb.tile([P, T], I32, name="kw_win")
+        ks_win = sb.tile([P, T], U8, name="ks_win")
+        fac_rows = sb.tile([P, P], F32, name="fac_rows")
+        ident = sb.tile([P, P], F32, name="ident")
+
+        nc.vector.memset(ks_win[:].bitcast(I32), 0)
+        nc.gpsimd.memset(fac_rows[:], 0.0)
+        make_identity(nc, ident[:])
+        for j in range(BLOCKS):
+            eng = nc.vector if j < 2 else nc.gpsimd
+            eng.memset(lo_win[j][:, U:], 0.0)
+            eng.memset(hi_win[j][:, U:], 0.0)
+
+        def load_lo(j):
+            nc.sync.dma_start(lo_win[j][:, 0:U], low[j * P : (j + 1) * P, :])
+
+        def load_hi(j):
+            nc.sync.dma_start(hi_win[j][:, 0:U], high[j * P : (j + 1) * P, :])
+
+        def load_val(j):
+            nc.sync.dma_start(val_win[j][:], vals[j * P : (j + 1) * P, :])
+
+        nc.sync.dma_start(cls_list[:], offs2)
+        nc.sync.dma_start(tok_list[:], offs)
+        load_lo(0)
+        for g in range(4):
+            nc.sync.dma_start(ks_win[32 * g : 32 * g + 4, :].bitcast(I32), keys_scales[0, 4 * g : 4 * g + 4, :].bitcast(I32))
+        nc.sync.dma_start(kw_win[:], keys_words[0].rearrange("p n t -> p (n t)").bitcast(I32))
+        load_hi(0)
+        nc.sync.dma_start(q_raw[:], query.rearrange("(p j) q -> p j q", j=4))
+        load_lo(1)
+        load_val(0)
+        load_hi(1)
+        nc.sync.dma_start(fac_rows[0:4, :].rearrange("t (b r) -> t b r", r=8), vsc[:, 0].rearrange("(b t r) -> t b r", t=4, r=8))
+        nc.sync.dma_start(fac_rows[4:8, :].rearrange("t (b r) -> t b r", r=8), size[0, :].rearrange("(b t r) -> t b r", t=4, r=8))
+        load_val(1)
+        load_lo(2)
+        load_hi(2)
+        load_val(2)
+        load_lo(3)
+        load_val(3)
+        load_hi(3)
+
+        fac = sb.tile([P, 8], F32, name="fac")
+
+        lo_g = [sb.tile([P, I], F32, name=f"lo_g{j}") for j in range(BLOCKS)]
+        hi_g = [sb.tile([P, I], F32, name=f"hi_g{j}") for j in range(BLOCKS)]
+        val_g = [sb.tile([P, I], F32, name=f"val_g{j}") for j in range(BLOCKS)]
+        raised = [sb.tile([P, I], F32, name=f"raised{j}") for j in range(BLOCKS)]
+        bounded = [sb.tile([P, I], F32, name=f"bounded{j}") for j in range(BLOCKS)]
+        vv_bf = [sb.tile([P, P, 4], BF16, name=f"vv_bf{j}", align_bytes=64) for j in range(BLOCKS)]
+        vv_w = [sb.tile([P, P], U32, name=f"vv_w{j}", align_bytes=64) for j in range(BLOCKS)]
+        vv_s = [sb.tile([P, P], U8, name=f"vv_s{j}", align_bytes=64) for j in range(BLOCKS)]
+
+        def gather_lo(j):
+            nc.scalar.activation(lo_g[j][:], lo_win[j][:].indirect(cls_list[:]), ACT.Copy)
+
+        def gather_hi(j):
+            nc.scalar.activation(hi_g[j][:], hi_win[j][:].indirect(cls_list[:]), ACT.Copy)
+
+        def gather_val_v(j):
+            n = VALS_ON_VECTOR[j]
+            nc.vector.tensor_copy(val_g[j][:, 0:n], val_win[j][:].indirect(tok_list[:, 0 : n // 16]))
+
+        def gather_val_s(j):
+            n = VALS_ON_VECTOR[j]
+            nc.scalar.activation(val_g[j][:, n:I], val_win[j][:].indirect(tok_list[:, n // 16 : I // 16]), ACT.Copy)
+
+        def turn(src, bank):
+            for t in range(4):
+                nc.tensor.transpose(bank[:, t, :], src[:, t * P : (t + 1) * P], ident[:])
+
+        def scale_out(bank, factor, dst):
+            nc.vector.tensor_tensor(dst[:], bank[:].rearrange("p t c -> p c t"), factor.unsqueeze(1).to_broadcast([P, P, 4]), ALU.mult)
+
+        def quantise(src, words, scales):
+            nc.vector.quantize_mx(out=words[:].bitcast(FP8X4), scales=scales[:], in_=src[:].rearrange("p c t -> p (c t)"))
+
+        banks = {}
+
+        def raise_block(j):
+            nc.vector.tensor_tensor(raised[j][:], val_g[j][:], lo_g[j][:], ALU.max)
+
+        def cap_block(j):
+            nc.vector.tensor_tensor(dealt(bounded[j][:]), natural(raised[j][:]), natural(hi_g[j][:]), ALU.min)
+            banks[j] = ps_turn.tile([P, 4, P], F32, name="turn")
+            turn(bounded[j], banks[j])
+
+        def scale_block(j):
+            scale_out(banks[j], fac[:, 0:4], vv_bf[j])
+
+        def quantise_block(j):
+            quantise(vv_bf[j], vv_w[j], vv_s[j])
+
+        kw_g = sb.tile([P, I], U32, name="kw_g", align_bytes=64)
+        ks_g = sb.tile([P, I], U8, name="ks_g", align_bytes=64)
+        q_bf = sb.tile([P, Q, 4], BF16, name="q_bf", align_bytes=64)
+        q_w = sb.tile([P, Q], U32, name="q_w", align_bytes=64)
+        q_s = sb.tile([P, Q], U8, name="q_s", align_bytes=64)
+        neg_max = sb.tile([P, 1], F32, name="neg_max")
+        row_sum = sb.tile([P, 1], F32, name="row_sum")
+        inv_sum = sb.tile([P, 1], F32, name="inv_sum")
+        p_exp = sb.tile([P, I], F32, name="p_exp")
+        p_norm = sb.tile([P, I], F32, name="p_norm")
+        w_bf = sb.tile([P, Q, 4], BF16, name="w_bf", align_bytes=64)
+        w_w = sb.tile([P, Q], U32, name="w_w", align_bytes=64)
+        w_s = sb.tile([P, Q], U8, name="w_s", align_bytes=64)
+
+        gather_lo(0)
+        gather_hi(0)
+        nc.vector.tensor_copy(ks_g[:], ks_win[:].indirect(tok_list[:]))
+        nc.vector.tensor_copy(kw_g[:], kw_win[:].bitcast(U32).indirect(tok_list[:]))
+        nc.vector.tensor_copy(q_bf[:], q_raw[:].rearrange("p j q -> p q j"))
+        quantise(q_bf, q_w, q_s)
+        scores = ps.tile([P, I], F32, name="scores")
+        nc.tensor.matmul_mx(out=scores[:], lhsT=q_w[:].bitcast(FP8X4), lhsT_scale=q_s[:], rhs=kw_g[:].bitcast(FP8X4), rhs_scale=ks_g[:], start=True, stop=True)
+        gather_lo(1)
+        gather_val_v(0)
+        gather_hi(1)
+        nc.vector.tensor_reduce(neg_max[:], scores[:], mybir.AxisListType.X, ALU.max, negate=True)
+        nc.scalar.activation(dealt(p_exp[:]), natural(scores[:]), ACT.Exp, bias=neg_max[:], accum_out=row_sum[:])
+        fac_ps = ps.tile([P, P], F32, name="fac_ps")
+        nc.tensor.transpose(fac_ps[:], fac_rows[:], ident[:])
+        nc.scalar.copy(fac[:], fac_ps[:, 0:8])
+        gather_val_s(1)
+        raise_block(0)
+        nc.vector.reciprocal(inv_sum[:], row_sum[:])
+        cap_block(0)
+        nc.vector.tensor_scalar(p_norm[:], p_exp[:], inv_sum[:], None, ALU.mult)
+        w_ps = ps.tile([P, 4, Q], F32, name="w_ps")
+        turn(p_norm, w_ps)
+        gather_lo(2)
+        gather_hi(2)
+        raise_block(1)
+        scale_block(0)
+        cap_block(1)
+        quantise_block(0)
+        scale_out(w_ps, fac[:, 4:8], w_bf)
+        gather_val_v(2)
+        quantise(w_bf, w_w, w_s)
+        gather_lo(3)
+        gather_val_s(3)
+        gather_hi(3)
+        raise_block(2)
+        scale_block(1)
+        cap_block(2)
+        quantise_block(1)
+        raise_block(3)
+        scale_block(2)
+        cap_block(3)
+        quantise_block(2)
+        scale_block(3)
+        quantise_block(3)
+
+        for name, blocks in (("a", range(0, BLOCKS - 1)), ("b", range(BLOCKS - 1, BLOCKS))):
+            width = len(blocks) * P
+            acc = ps.tile([P, width], F32, name="acc_" + name)
+            for n, j in enumerate(blocks):
+                nc.tensor.matmul_mx(out=acc[:, n * P : (n + 1) * P], lhsT=w_w[:].bitcast(FP8X4), lhsT_scale=w_s[:], rhs=vv_w[j][:].bitcast(FP8X4), rhs_scale=vv_s[j][:], start=True, stop=True)
+            res = sb.tile([P, width], F32, name="res_" + name)
+            nc.scalar.copy(res[:], acc[:])
+            nc.sync.dma_start(out[:, blocks[0] * P : blocks[0] * P + width], res[:])

@@ -17,8 +17,7 @@ P = 128
 D, T, I, Q, E, U = 512, 1024, 512, 128, 512, 256
 FLOPS = 2 * D * Q * I + 2 * I * Q * E
 BLOCKS = E // P
-BOUND_W = I + 8
-VALS_ON_VECTOR = (512, 0, 512, 0)
+BOUND_W = I + 16
 
 
 def tile_attend_boundedvalues_kernel(tc, query, keys_words, keys_scales, size, vals, low, high, vsc, offs, offs2, out):
@@ -34,16 +33,19 @@ def tile_attend_boundedvalues_kernel(tc, query, keys_words, keys_scales, size, v
         def natural(ap):
             return ap.rearrange("p (b t r) -> p b t r", t=4, r=8)
 
+        def tile(shape, dtype, name, on=None):
+            return sb.tile(shape, dtype, name=name, tag=on or name, align_bytes=64)
+
         tok_list = sb.tile([P, I // 16], U16, name="tok_list")
         cls_list = sb.tile([P, I // 16], U16, name="cls_list")
-        lo_win = [sb.tile([P, BOUND_W], F32, name=f"lo_win{j}") for j in range(BLOCKS)]
-        hi_win = [sb.tile([P, BOUND_W], F32, name=f"hi_win{j}") for j in range(BLOCKS)]
-        val_win = [sb.tile([P, T], F32, name=f"val_win{j}") for j in range(BLOCKS)]
-        q_raw = sb.tile([P, 4, Q], F32, name="q_raw")
-        kw_win = sb.tile([P, T], I32, name="kw_win")
-        ks_win = sb.tile([P, T], U8, name="ks_win")
-        fac_rows = sb.tile([P, P], F32, name="fac_rows")
-        ident = sb.tile([P, P], F32, name="ident")
+        lo_win = [tile([P, BOUND_W], F32, f"lo_win{j}") for j in range(BLOCKS)]
+        hi_win = [tile([P, BOUND_W], F32, f"hi_win{j}") for j in range(BLOCKS)]
+        val_win = [tile([P, T], F32, f"val_win{j}") for j in range(BLOCKS)]
+        q_raw = tile([P, 4, Q], F32, "q_raw")
+        kw_win = tile([P, T], I32, "kw_win")
+        ks_win = tile([P, T], U8, "ks_win")
+        fac_rows = tile([P, P], F32, "fac_rows")
+        ident = tile([P, P], F32, "ident")
 
         nc.vector.memset(ks_win[:].bitcast(I32), 0)
         nc.gpsimd.memset(fac_rows[:], 0.0)
@@ -62,37 +64,30 @@ def tile_attend_boundedvalues_kernel(tc, query, keys_words, keys_scales, size, v
         def load_val(j):
             nc.sync.dma_start(val_win[j][:], vals[j * P : (j + 1) * P, :])
 
+        nc.sync.dma_start(q_raw[:], query.rearrange("(p j) q -> p j q", j=4))
         nc.sync.dma_start(cls_list[:], offs2)
-        nc.sync.dma_start(tok_list[:], offs)
         load_lo(0)
+        load_hi(0)
+        nc.sync.dma_start(tok_list[:], offs)
+        nc.sync.dma_start(kw_win[:], keys_words[0].rearrange("p n t -> p (n t)").bitcast(I32))
+        load_lo(1)
+        load_hi(1)
         for g in range(4):
             nc.sync.dma_start(ks_win[32 * g : 32 * g + 4, :].bitcast(I32), keys_scales[0, 4 * g : 4 * g + 4, :].bitcast(I32))
-        nc.sync.dma_start(kw_win[:], keys_words[0].rearrange("p n t -> p (n t)").bitcast(I32))
-        load_hi(0)
-        nc.sync.dma_start(q_raw[:], query.rearrange("(p j) q -> p j q", j=4))
-        load_lo(1)
         load_val(0)
-        load_hi(1)
+        load_lo(2)
         nc.sync.dma_start(fac_rows[0:4, :].rearrange("t (b r) -> t b r", r=8), vsc[:, 0].rearrange("(b t r) -> t b r", t=4, r=8))
         nc.sync.dma_start(fac_rows[4:8, :].rearrange("t (b r) -> t b r", r=8), size[0, :].rearrange("(b t r) -> t b r", t=4, r=8))
         load_val(1)
-        load_lo(2)
         load_hi(2)
         load_val(2)
         load_lo(3)
         load_val(3)
         load_hi(3)
 
-        fac = sb.tile([P, 8], F32, name="fac")
-
-        lo_g = [sb.tile([P, I], F32, name=f"lo_g{j}") for j in range(BLOCKS)]
-        hi_g = [sb.tile([P, I], F32, name=f"hi_g{j}") for j in range(BLOCKS)]
-        val_g = [sb.tile([P, I], F32, name=f"val_g{j}") for j in range(BLOCKS)]
-        raised = [sb.tile([P, I], F32, name=f"raised{j}") for j in range(BLOCKS)]
-        bounded = [sb.tile([P, I], F32, name=f"bounded{j}") for j in range(BLOCKS)]
-        vv_bf = [sb.tile([P, P, 4], BF16, name=f"vv_bf{j}", align_bytes=64) for j in range(BLOCKS)]
-        vv_w = [sb.tile([P, P], U32, name=f"vv_w{j}", align_bytes=64) for j in range(BLOCKS)]
-        vv_s = [sb.tile([P, P], U8, name=f"vv_s{j}", align_bytes=64) for j in range(BLOCKS)]
+        lo_g = [tile([P, I], F32, f"lo_g{j}") for j in range(BLOCKS)]
+        hi_g = [tile([P, I], F32, f"hi_g{j}") for j in range(BLOCKS)]
+        val_g = [tile([P, I], F32, f"val_g{j}") for j in range(BLOCKS)]
 
         def gather_lo(j):
             nc.scalar.activation(lo_g[j][:], lo_win[j][:].indirect(cls_list[:]), ACT.Copy)
@@ -100,105 +95,111 @@ def tile_attend_boundedvalues_kernel(tc, query, keys_words, keys_scales, size, v
         def gather_hi(j):
             nc.scalar.activation(hi_g[j][:], hi_win[j][:].indirect(cls_list[:]), ACT.Copy)
 
-        def gather_val_v(j):
-            n = VALS_ON_VECTOR[j]
-            nc.vector.tensor_copy(val_g[j][:, 0:n], val_win[j][:].indirect(tok_list[:, 0 : n // 16]))
-
-        def gather_val_s(j):
-            n = VALS_ON_VECTOR[j]
-            nc.scalar.activation(val_g[j][:, n:I], val_win[j][:].indirect(tok_list[:, n // 16 : I // 16]), ACT.Copy)
+        def gather_val(j):
+            nc.scalar.activation(val_g[j][:], val_win[j][:].indirect(tok_list[:]), ACT.Copy)
 
         def turn(src, bank):
             for t in range(4):
                 nc.tensor.transpose(bank[:, t, :], src[:, t * P : (t + 1) * P], ident[:])
 
         def scale_out(bank, factor, dst):
-            nc.vector.tensor_tensor(dst[:], bank[:].rearrange("p t c -> p c t"), factor.unsqueeze(1).to_broadcast([P, P, 4]), ALU.mult)
+            nc.vector.tensor_tensor(dst.rearrange("p (c t) -> p c t", t=4), bank[:].rearrange("p t c -> p c t"), factor.unsqueeze(1).to_broadcast([P, P, 4]), ALU.mult)
 
         def quantise(src, words, scales):
-            nc.vector.quantize_mx(out=words[:].bitcast(FP8X4), scales=scales[:], in_=src[:].rearrange("p c t -> p (c t)"))
+            nc.vector.quantize_mx(out=words.bitcast(FP8X4), scales=scales, in_=src)
 
-        banks = {}
+        def raise_block(j, raised):
+            nc.vector.tensor_tensor(raised, val_g[j][:], lo_g[j][:], ALU.max)
 
-        def raise_block(j):
-            nc.vector.tensor_tensor(raised[j][:], val_g[j][:], lo_g[j][:], ALU.max)
+        def cap_block(j, raised, bounded, pieces=1):
+            bank = ps_turn.tile([P, 4, P], F32, name="turn")
+            n = 4 // pieces
+            for t0 in range(0, 4, n):
+                ts = slice(t0, t0 + n)
+                nc.vector.tensor_tensor(dealt(bounded)[:, :, ts, :], natural(raised)[:, :, ts, :], natural(hi_g[j][:])[:, :, ts, :], ALU.min)
+            turn(bounded, bank)
+            return bank
 
-        def cap_block(j):
-            nc.vector.tensor_tensor(dealt(bounded[j][:]), natural(raised[j][:]), natural(hi_g[j][:]), ALU.min)
-            banks[j] = ps_turn.tile([P, 4, P], F32, name="turn")
-            turn(bounded[j], banks[j])
+        def finish(e0, words, scales, bank_tag, res):
+            width = words.shape[1]
+            acc = ps.tile([P, width], F32, name=f"acc{e0}", tag=bank_tag)
+            nc.tensor.matmul_mx(out=acc[:], lhsT=w_w[:].bitcast(FP8X4), lhsT_scale=w_s[:], rhs=words.bitcast(FP8X4), rhs_scale=scales, start=True, stop=True)
+            nc.scalar.copy(res, acc[:])
+            nc.sync.dma_start(out[:, e0 : e0 + width], res)
 
-        def scale_block(j):
-            scale_out(banks[j], fac[:, 0:4], vv_bf[j])
+        kw_g = tile([P, I], U32, "kw_g")
+        ks_g = tile([P, I], U8, "ks_g")
+        q_bf = tile([P, 4 * Q], BF16, "q_bf")
+        q_w = tile([P, Q], U32, "q_w")
+        q_s = tile([P, Q], U8, "q_s")
+        row_sum = tile([P, 1], F32, "row_sum")
+        inv_sum = tile([P, 1], F32, "inv_sum")
+        p_norm = tile([P, I], F32, "p_norm")
+        w_s = tile([P, Q], U8, "w_s")
+        fac = tile([P, 8], F32, "fac")
+        vv_s = tile([P, E], U8, "vv_s")
 
-        def quantise_block(j):
-            quantise(vv_bf[j], vv_w[j], vv_s[j])
-
-        kw_g = sb.tile([P, I], U32, name="kw_g", align_bytes=64)
-        ks_g = sb.tile([P, I], U8, name="ks_g", align_bytes=64)
-        q_bf = sb.tile([P, Q, 4], BF16, name="q_bf", align_bytes=64)
-        q_w = sb.tile([P, Q], U32, name="q_w", align_bytes=64)
-        q_s = sb.tile([P, Q], U8, name="q_s", align_bytes=64)
-        neg_max = sb.tile([P, 1], F32, name="neg_max")
-        row_sum = sb.tile([P, 1], F32, name="row_sum")
-        inv_sum = sb.tile([P, 1], F32, name="inv_sum")
-        p_exp = sb.tile([P, I], F32, name="p_exp")
-        p_norm = sb.tile([P, I], F32, name="p_norm")
-        w_bf = sb.tile([P, Q, 4], BF16, name="w_bf", align_bytes=64)
-        w_w = sb.tile([P, Q], U32, name="w_w", align_bytes=64)
-        w_s = sb.tile([P, Q], U8, name="w_s", align_bytes=64)
-
-        gather_lo(0)
+        nc.scalar.activation(q_bf[:].rearrange("p (q j) -> p q j", j=4), q_raw[:].rearrange("p j q -> p q j"), ACT.Copy)
+        for h in range(2):
+            nc.vector.tensor_copy(lo_g[0][:, h * 256 : (h + 1) * 256], lo_win[0][:].indirect(cls_list[:, h * 16 : (h + 1) * 16]))
         gather_hi(0)
-        nc.vector.tensor_copy(ks_g[:], ks_win[:].indirect(tok_list[:]))
+        quantise(q_bf[:], q_w[:], q_s[:])
         nc.vector.tensor_copy(kw_g[:], kw_win[:].bitcast(U32).indirect(tok_list[:]))
-        nc.vector.tensor_copy(q_bf[:], q_raw[:].rearrange("p j q -> p q j"))
-        quantise(q_bf, q_w, q_s)
-        scores = ps.tile([P, I], F32, name="scores")
-        nc.tensor.matmul_mx(out=scores[:], lhsT=q_w[:].bitcast(FP8X4), lhsT_scale=q_s[:], rhs=kw_g[:].bitcast(FP8X4), rhs_scale=ks_g[:], start=True, stop=True)
         gather_lo(1)
-        gather_val_v(0)
         gather_hi(1)
-        nc.vector.tensor_reduce(neg_max[:], scores[:], mybir.AxisListType.X, ALU.max, negate=True)
-        nc.scalar.activation(dealt(p_exp[:]), natural(scores[:]), ACT.Exp, bias=neg_max[:], accum_out=row_sum[:])
-        fac_ps = ps.tile([P, P], F32, name="fac_ps")
-        nc.tensor.transpose(fac_ps[:], fac_rows[:], ident[:])
-        nc.scalar.copy(fac[:], fac_ps[:, 0:8])
-        gather_val_s(1)
-        raise_block(0)
-        nc.vector.reciprocal(inv_sum[:], row_sum[:])
-        cap_block(0)
-        nc.vector.tensor_scalar(p_norm[:], p_exp[:], inv_sum[:], None, ALU.mult)
-        w_ps = ps.tile([P, 4, Q], F32, name="w_ps")
-        turn(p_norm, w_ps)
+        nc.vector.tensor_copy(ks_g[:], ks_win[:].indirect(tok_list[:]))
+        scores = ps.tile([P, I], F32, name="scores", tag="scores")
+        nc.tensor.matmul_mx(out=scores[:], lhsT=q_w[:].bitcast(FP8X4), lhsT_scale=q_s[:], rhs=kw_g[:].bitcast(FP8X4), rhs_scale=ks_g[:], start=True, stop=True)
+        nc.vector.tensor_copy(val_g[0][:], val_win[0][:].indirect(tok_list[:]))
         gather_lo(2)
+        after_lo2 = tile([P, I + 1], F32, "after_lo2", on="lo_win2")
+        raised0, neg_max = after_lo2[:, 0:I], after_lo2[:, I : I + 1]
+        nc.vector.tensor_reduce(neg_max, scores[:], mybir.AxisListType.X, ALU.max, negate=True)
+        raise_block(0, raised0)
+        fac_ps = ps.tile([P, P], F32, name="fac_ps", tag="fac_ps")
+        nc.tensor.transpose(fac_ps[:], fac_rows[:], ident[:])
+        nc.vector.tensor_copy(fac[:], fac_ps[:, 0:8])
+        gather_val(1)
+        after_val1 = tile([P, 2 * I], F32, "after_val1", on="val_win1")
+        bounded0, p_exp = after_val1[:, 0:I], after_val1[:, I : 2 * I]
+        nc.scalar.activation(dealt(p_exp), natural(scores[:]), ACT.Exp, bias=neg_max, accum_out=row_sum[:])
         gather_hi(2)
-        raise_block(1)
-        scale_block(0)
-        cap_block(1)
-        quantise_block(0)
-        scale_out(w_ps, fac[:, 4:8], w_bf)
-        gather_val_v(2)
-        quantise(w_bf, w_w, w_s)
+        gather_val(2)
         gather_lo(3)
-        gather_val_s(3)
+        gather_val(3)
         gather_hi(3)
-        raise_block(2)
-        scale_block(1)
-        cap_block(2)
-        quantise_block(1)
-        raise_block(3)
-        scale_block(2)
-        cap_block(3)
-        quantise_block(2)
-        scale_block(3)
-        quantise_block(3)
 
-        for name, blocks in (("a", range(0, BLOCKS - 1)), ("b", range(BLOCKS - 1, BLOCKS))):
-            width = len(blocks) * P
-            acc = ps.tile([P, width], F32, name="acc_" + name)
-            for n, j in enumerate(blocks):
-                nc.tensor.matmul_mx(out=acc[:, n * P : (n + 1) * P], lhsT=w_w[:].bitcast(FP8X4), lhsT_scale=w_s[:], rhs=vv_w[j][:].bitcast(FP8X4), rhs_scale=vv_s[j][:], start=True, stop=True)
-            res = sb.tile([P, width], F32, name="res_" + name)
-            nc.scalar.copy(res[:], acc[:])
-            nc.sync.dma_start(out[:, blocks[0] * P : blocks[0] * P + width], res[:])
+        raised = [None] + [tile([P, I], F32, f"raised{j}") for j in range(1, BLOCKS)]
+        bounded = [None] + [tile([P, I], F32, f"bounded{j}") for j in range(1, BLOCKS)]
+        raise_block(1, raised[1][:])
+        bank0 = cap_block(0, raised0, bounded0)
+        nc.vector.reciprocal(inv_sum[:], row_sum[:])
+        bank1 = cap_block(1, raised[1][:], bounded[1][:])
+        nc.vector.tensor_scalar(p_norm[:], p_exp, inv_sum[:], None, ALU.mult)
+        w_ps = ps.tile([P, 4, Q], F32, name="w_ps", tag="w_ps")
+        turn(p_norm, w_ps)
+        vv01 = tile([P, 2 * I], BF16, "vv01")
+        scale_out(bank0, fac[:, 0:4], vv01[:, 0:I])
+        scale_out(bank1, fac[:, 0:4], vv01[:, I : 2 * I])
+        raise_block(2, raised[2][:])
+        vv01_w = tile([P, 2 * P], U32, "vv01_w", on="val_win2")
+        quantise(vv01[:], vv01_w[:], vv_s[:, 0 : 2 * P])
+        bank2 = cap_block(2, raised[2][:], bounded[2][:])
+        w_bf = tile([P, 4 * Q], BF16, "w_bf", on="lo_win3")
+        scale_out(w_ps, fac[:, 4:8], w_bf[:])
+        raise_block(3, raised[3][:])
+        w_w = tile([P, Q], U32, "w_w", on="val_win3")
+        quantise(w_bf[:], w_w[:], w_s[:])
+        after_hi3 = tile([P, 2 * I], BF16, "after_hi3", on="hi_win3")
+        vv2, res01 = after_hi3[:, 0:I], after_hi3[:, I : 2 * I].bitcast(F32)
+        finish(0, vv01_w[:], vv_s[:, 0 : 2 * P], "scores", res01)
+        bank3 = cap_block(3, raised[3][:], bounded[3][:], pieces=2)
+        vv23_w = tile([P, 2 * P], U32, "vv23_w")
+        vv3 = tile([P, I], BF16, "vv3")
+        res23 = tile([P, 2 * P], F32, "res23")
+        scale_out(bank2, fac[:, 0:4], vv2)
+        quantise(vv2, vv23_w[:, 0:P], vv_s[:, 2 * P : 3 * P])
+        scale_out(bank3, fac[:, 0:4], vv3[:])
+        finish(2 * P, vv23_w[:, 0:P], vv_s[:, 2 * P : 3 * P], "fac_ps", res23[:, 0:P])
+        quantise(vv3[:], vv23_w[:, P : 2 * P], vv_s[:, 3 * P : 4 * P])
+        finish(3 * P, vv23_w[:, P : 2 * P], vv_s[:, 3 * P : 4 * P], "w_ps", res23[:, P : 2 * P])

@@ -18,6 +18,7 @@ D, T, I, Q, E, U = 512, 1024, 512, 128, 512, 256
 FLOPS = 2 * D * Q * I + 2 * I * Q * E
 BLOCKS = E // P
 BOUND_W = I + 16
+LO3_ON_VECTOR = 256
 
 
 def tile_attend_boundedvalues_kernel(tc, query, keys_words, keys_scales, size, vals, low, high, vsc, offs, offs2, out):
@@ -25,7 +26,6 @@ def tile_attend_boundedvalues_kernel(tc, query, keys_words, keys_scales, size, v
     with ExitStack() as ctx:
         sb = ctx.enter_context(tc.tile_pool(name="sb", bufs=1))
         ps = ctx.enter_context(tc.psum_pool(name="ps", bufs=1))
-        ps_turn = ctx.enter_context(tc.psum_pool(name="ps_turn", bufs=3))
 
         def dealt(ap):
             return ap.rearrange("p (t b r) -> p b t r", t=4, r=8)
@@ -64,23 +64,23 @@ def tile_attend_boundedvalues_kernel(tc, query, keys_words, keys_scales, size, v
         def load_val(j):
             nc.sync.dma_start(val_win[j][:], vals[j * P : (j + 1) * P, :])
 
-        nc.sync.dma_start(q_raw[:], query.rearrange("(p j) q -> p j q", j=4))
         nc.sync.dma_start(cls_list[:], offs2)
         load_lo(0)
+        nc.sync.dma_start(q_raw[:], query.rearrange("(p j) q -> p j q", j=4))
         load_hi(0)
-        nc.sync.dma_start(tok_list[:], offs)
-        nc.sync.dma_start(kw_win[:], keys_words[0].rearrange("p n t -> p (n t)").bitcast(I32))
         load_lo(1)
         load_hi(1)
+        nc.sync.dma_start(tok_list[:], offs)
+        nc.sync.dma_start(kw_win[:], keys_words[0].rearrange("p n t -> p (n t)").bitcast(I32))
+        load_val(0)
         for g in range(4):
             nc.sync.dma_start(ks_win[32 * g : 32 * g + 4, :].bitcast(I32), keys_scales[0, 4 * g : 4 * g + 4, :].bitcast(I32))
-        load_val(0)
+        load_val(1)
         load_lo(2)
         nc.sync.dma_start(fac_rows[0:4, :].rearrange("t (b r) -> t b r", r=8), vsc[:, 0].rearrange("(b t r) -> t b r", t=4, r=8))
         nc.sync.dma_start(fac_rows[4:8, :].rearrange("t (b r) -> t b r", r=8), size[0, :].rearrange("(b t r) -> t b r", t=4, r=8))
-        load_val(1)
-        load_hi(2)
         load_val(2)
+        load_hi(2)
         load_lo(3)
         load_val(3)
         load_hi(3)
@@ -112,7 +112,7 @@ def tile_attend_boundedvalues_kernel(tc, query, keys_words, keys_scales, size, v
             nc.vector.tensor_tensor(raised, val_g[j][:], lo_g[j][:], ALU.max)
 
         def cap_block(j, raised, bounded, pieces=1):
-            bank = ps_turn.tile([P, 4, P], F32, name="turn")
+            bank = ps.tile([P, 4, P], F32, name=f"turned{j}", tag=f"turn{j % 3}")
             n = 4 // pieces
             for t0 in range(0, 4, n):
                 ts = slice(t0, t0 + n)
@@ -120,12 +120,14 @@ def tile_attend_boundedvalues_kernel(tc, query, keys_words, keys_scales, size, v
             turn(bounded, bank)
             return bank
 
-        def finish(e0, words, scales, bank_tag, res):
-            width = words.shape[1]
-            acc = ps.tile([P, width], F32, name=f"acc{e0}", tag=bank_tag)
-            nc.tensor.matmul_mx(out=acc[:], lhsT=w_w[:].bitcast(FP8X4), lhsT_scale=w_s[:], rhs=words.bitcast(FP8X4), rhs_scale=scales, start=True, stop=True)
-            nc.scalar.copy(res, acc[:])
-            nc.sync.dma_start(out[:, e0 : e0 + width], res)
+        def multiply(acc, words, scales):
+            nc.tensor.matmul_mx(out=acc, lhsT=w_w[:].bitcast(FP8X4), lhsT_scale=w_s[:], rhs=words.bitcast(FP8X4), rhs_scale=scales, start=True, stop=True)
+
+        def store(e0, acc):
+            width = acc.shape[1]
+            res = tile([P, width], F32, f"res{e0}")
+            nc.scalar.copy(res[:], acc)
+            nc.sync.dma_start(out[:, e0 : e0 + width], res[:])
 
         kw_g = tile([P, I], U32, "kw_g")
         ks_g = tile([P, I], U8, "ks_g")
@@ -139,67 +141,74 @@ def tile_attend_boundedvalues_kernel(tc, query, keys_words, keys_scales, size, v
         fac = tile([P, 8], F32, "fac")
         vv_s = tile([P, E], U8, "vv_s")
 
+        def gather_halves_on_vector(dst, win):
+            for h in range(2):
+                nc.vector.tensor_copy(dst[:, h * 256 : (h + 1) * 256], win[:].indirect(cls_list[:, h * 16 : (h + 1) * 16]))
+
+        gather_halves_on_vector(lo_g[0], lo_win[0])
         nc.scalar.activation(q_bf[:].rearrange("p (q j) -> p q j", j=4), q_raw[:].rearrange("p j q -> p q j"), ACT.Copy)
-        for h in range(2):
-            nc.vector.tensor_copy(lo_g[0][:, h * 256 : (h + 1) * 256], lo_win[0][:].indirect(cls_list[:, h * 16 : (h + 1) * 16]))
-        gather_hi(0)
-        quantise(q_bf[:], q_w[:], q_s[:])
-        nc.vector.tensor_copy(kw_g[:], kw_win[:].bitcast(U32).indirect(tok_list[:]))
+        gather_halves_on_vector(hi_g[0], hi_win[0])
         gather_lo(1)
         gather_hi(1)
+        gather_val(0)
+        quantise(q_bf[:], q_w[:], q_s[:])
+        nc.vector.tensor_copy(kw_g[:], kw_win[:].bitcast(U32).indirect(tok_list[:]))
         nc.vector.tensor_copy(ks_g[:], ks_win[:].indirect(tok_list[:]))
         scores = ps.tile([P, I], F32, name="scores", tag="scores")
         nc.tensor.matmul_mx(out=scores[:], lhsT=q_w[:].bitcast(FP8X4), lhsT_scale=q_s[:], rhs=kw_g[:].bitcast(FP8X4), rhs_scale=ks_g[:], start=True, stop=True)
-        nc.vector.tensor_copy(val_g[0][:], val_win[0][:].indirect(tok_list[:]))
-        gather_lo(2)
-        after_lo2 = tile([P, I + 1], F32, "after_lo2", on="lo_win2")
-        raised0, neg_max = after_lo2[:, 0:I], after_lo2[:, I : I + 1]
-        nc.vector.tensor_reduce(neg_max, scores[:], mybir.AxisListType.X, ALU.max, negate=True)
-        raise_block(0, raised0)
-        fac_ps = ps.tile([P, P], F32, name="fac_ps", tag="fac_ps")
-        nc.tensor.transpose(fac_ps[:], fac_rows[:], ident[:])
-        nc.vector.tensor_copy(fac[:], fac_ps[:, 0:8])
+        raised = [tile([P, I], F32, f"raised{j}", on="ks_win" if j == 0 else None) for j in range(BLOCKS)]
+        raise_block(0, raised[0][:])
+        neg_max = tile([P, 1], F32, "neg_max")
+        nc.vector.tensor_reduce(neg_max[:], scores[:], mybir.AxisListType.X, ALU.max, negate=True)
         gather_val(1)
-        after_val1 = tile([P, 2 * I], F32, "after_val1", on="val_win1")
-        bounded0, p_exp = after_val1[:, 0:I], after_val1[:, I : 2 * I]
-        nc.scalar.activation(dealt(p_exp), natural(scores[:]), ACT.Exp, bias=neg_max, accum_out=row_sum[:])
-        gather_hi(2)
+        gather_lo(2)
+        p_exp = tile([P, I], F32, "p_exp", on="lo_win2")
+        nc.scalar.activation(dealt(p_exp[:]), natural(scores[:]), ACT.Exp, bias=neg_max[:], accum_out=row_sum[:])
         gather_val(2)
-        gather_lo(3)
+        gather_hi(2)
+        n = LO3_ON_VECTOR
+        nc.scalar.activation(lo_g[3][:, n:I], lo_win[3][:].indirect(cls_list[:, n // 16 : I // 16]), ACT.Copy)
         gather_val(3)
         gather_hi(3)
 
-        raised = [None] + [tile([P, I], F32, f"raised{j}") for j in range(1, BLOCKS)]
-        bounded = [None] + [tile([P, I], F32, f"bounded{j}") for j in range(1, BLOCKS)]
+        bounded = [tile([P, I], F32, f"bounded{j}", on="val_win1" if j == 0 else None) for j in range(BLOCKS)]
+        fac_ps = ps.tile([P, P], F32, name="fac_ps", tag="fac_ps")
+        nc.tensor.transpose(fac_ps[:], fac_rows[:], ident[:])
         raise_block(1, raised[1][:])
-        bank0 = cap_block(0, raised0, bounded0)
-        nc.vector.reciprocal(inv_sum[:], row_sum[:])
+        bank0 = cap_block(0, raised[0][:], bounded[0][:])
         bank1 = cap_block(1, raised[1][:], bounded[1][:])
-        nc.vector.tensor_scalar(p_norm[:], p_exp, inv_sum[:], None, ALU.mult)
+        nc.vector.reciprocal(inv_sum[:], row_sum[:])
+        nc.vector.tensor_copy(fac[:], fac_ps[:, 0:8])
+        nc.vector.tensor_scalar(p_norm[:], p_exp[:], inv_sum[:], None, ALU.mult)
         w_ps = ps.tile([P, 4, Q], F32, name="w_ps", tag="w_ps")
         turn(p_norm, w_ps)
-        vv01 = tile([P, 2 * I], BF16, "vv01")
-        scale_out(bank0, fac[:, 0:4], vv01[:, 0:I])
-        scale_out(bank1, fac[:, 0:4], vv01[:, I : 2 * I])
         raise_block(2, raised[2][:])
-        vv01_w = tile([P, 2 * P], U32, "vv01_w", on="val_win2")
-        quantise(vv01[:], vv01_w[:], vv_s[:, 0 : 2 * P])
+        vv0 = tile([P, I], BF16, "vv0", on="val_win2")
+        scale_out(bank0, fac[:, 0:4], vv0[:])
         bank2 = cap_block(2, raised[2][:], bounded[2][:])
-        w_bf = tile([P, 4 * Q], BF16, "w_bf", on="lo_win3")
-        scale_out(w_ps, fac[:, 4:8], w_bf[:])
+        after_hi2 = tile([P, 2 * I], BF16, "after_hi2", on="hi_win2")
+        vv1, w_bf = after_hi2[:, 0:I], after_hi2[:, I : 2 * I]
+        scale_out(bank1, fac[:, 0:4], vv1)
+        nc.vector.tensor_copy(lo_g[3][:, 0:n], lo_win[3][:].indirect(cls_list[:, 0 : n // 16]))
+        scale_out(w_ps, fac[:, 4:8], w_bf)
+        vv01_w = tile([P, 2 * P], U32, "vv01_w", on="lo_win3")
+        quantise(vv0[:], vv01_w[:, 0:P], vv_s[:, 0:P])
+        quantise(vv1, vv01_w[:, P : 2 * P], vv_s[:, P : 2 * P])
         raise_block(3, raised[3][:])
         w_w = tile([P, Q], U32, "w_w", on="val_win3")
-        quantise(w_bf[:], w_w[:], w_s[:])
-        after_hi3 = tile([P, 2 * I], BF16, "after_hi3", on="hi_win3")
-        vv2, res01 = after_hi3[:, 0:I], after_hi3[:, I : 2 * I].bitcast(F32)
-        finish(0, vv01_w[:], vv_s[:, 0 : 2 * P], "scores", res01)
+        quantise(w_bf, w_w[:], w_s[:])
         bank3 = cap_block(3, raised[3][:], bounded[3][:], pieces=2)
-        vv23_w = tile([P, 2 * P], U32, "vv23_w")
+        vv2 = tile([P, I], BF16, "vv2", on="hi_win3")
         vv3 = tile([P, I], BF16, "vv3")
-        res23 = tile([P, 2 * P], F32, "res23")
-        scale_out(bank2, fac[:, 0:4], vv2)
-        quantise(vv2, vv23_w[:, 0:P], vv_s[:, 2 * P : 3 * P])
+        vv23_w = tile([P, 2 * P], U32, "vv23_w")
+        scale_out(bank2, fac[:, 0:4], vv2[:])
+        quantise(vv2[:], vv23_w[:, 0:P], vv_s[:, 2 * P : 3 * P])
         scale_out(bank3, fac[:, 0:4], vv3[:])
-        finish(2 * P, vv23_w[:, 0:P], vv_s[:, 2 * P : 3 * P], "fac_ps", res23[:, 0:P])
+        acc012 = ps.tile([P, 3 * P], F32, name="acc012", tag="turn2")
+        multiply(acc012[:, 0 : 2 * P], vv01_w[:], vv_s[:, 0 : 2 * P])
+        multiply(acc012[:, 2 * P : 3 * P], vv23_w[:, 0:P], vv_s[:, 2 * P : 3 * P])
+        store(0, acc012[:])
         quantise(vv3[:], vv23_w[:, P : 2 * P], vv_s[:, 3 * P : 4 * P])
-        finish(3 * P, vv23_w[:, P : 2 * P], vv_s[:, 3 * P : 4 * P], "w_ps", res23[:, P : 2 * P])
+        acc3 = ps.tile([P, P], F32, name="acc3", tag="w_ps")
+        multiply(acc3[:], vv23_w[:, P : 2 * P], vv_s[:, 3 * P : 4 * P])
+        store(3 * P, acc3[:])

@@ -72,6 +72,7 @@ def tile_attend_boundedvalues_kernel(tc, query, keys_words, keys_scales, size, v
         load_hi(1)
         nc.sync.dma_start(tok_list[:], offs)
         nc.sync.dma_start(kw_win[:], keys_words[0].rearrange("p n t -> p (n t)").bitcast(I32))
+        load_lo(3)
         load_val(0)
         for g in range(4):
             nc.sync.dma_start(ks_win[32 * g : 32 * g + 4, :].bitcast(I32), keys_scales[0, 4 * g : 4 * g + 4, :].bitcast(I32))
@@ -81,7 +82,6 @@ def tile_attend_boundedvalues_kernel(tc, query, keys_words, keys_scales, size, v
         nc.sync.dma_start(fac_rows[4:8, :].rearrange("t (b r) -> t b r", r=8), size[0, :].rearrange("(b t r) -> t b r", t=4, r=8))
         load_val(2)
         load_hi(2)
-        load_lo(3)
         load_val(3)
         load_hi(3)
 
@@ -123,12 +123,6 @@ def tile_attend_boundedvalues_kernel(tc, query, keys_words, keys_scales, size, v
         def multiply(acc, words, scales):
             nc.tensor.matmul_mx(out=acc, lhsT=w_w[:].bitcast(FP8X4), lhsT_scale=w_s[:], rhs=words.bitcast(FP8X4), rhs_scale=scales, start=True, stop=True)
 
-        def store(e0, acc):
-            width = acc.shape[1]
-            res = tile([P, width], F32, f"res{e0}")
-            nc.scalar.copy(res[:], acc)
-            nc.sync.dma_start(out[:, e0 : e0 + width], res[:])
-
         kw_g = tile([P, I], U32, "kw_g")
         ks_g = tile([P, I], U8, "ks_g")
         q_bf = tile([P, 4 * Q], BF16, "q_bf")
@@ -150,9 +144,12 @@ def tile_attend_boundedvalues_kernel(tc, query, keys_words, keys_scales, size, v
         gather_halves_on_vector(hi_g[0], hi_win[0])
         gather_lo(1)
         gather_hi(1)
+        n = LO3_ON_VECTOR
+        nc.scalar.activation(lo_g[3][:, n:I], lo_win[3][:].indirect(cls_list[:, n // 16 : I // 16]), ACT.Copy)
         gather_val(0)
         quantise(q_bf[:], q_w[:], q_s[:])
         nc.vector.tensor_copy(kw_g[:], kw_win[:].bitcast(U32).indirect(tok_list[:]))
+        nc.vector.tensor_copy(lo_g[3][:, 0:n], lo_win[3][:].indirect(cls_list[:, 0 : n // 16]))
         nc.vector.tensor_copy(ks_g[:], ks_win[:].indirect(tok_list[:]))
         scores = ps.tile([P, I], F32, name="scores", tag="scores")
         nc.tensor.matmul_mx(out=scores[:], lhsT=q_w[:].bitcast(FP8X4), lhsT_scale=q_s[:], rhs=kw_g[:].bitcast(FP8X4), rhs_scale=ks_g[:], start=True, stop=True)
@@ -166,8 +163,6 @@ def tile_attend_boundedvalues_kernel(tc, query, keys_words, keys_scales, size, v
         nc.scalar.activation(dealt(p_exp[:]), natural(scores[:]), ACT.Exp, bias=neg_max[:], accum_out=row_sum[:])
         gather_val(2)
         gather_hi(2)
-        n = LO3_ON_VECTOR
-        nc.scalar.activation(lo_g[3][:, n:I], lo_win[3][:].indirect(cls_list[:, n // 16 : I // 16]), ACT.Copy)
         gather_val(3)
         gather_hi(3)
 
@@ -189,26 +184,30 @@ def tile_attend_boundedvalues_kernel(tc, query, keys_words, keys_scales, size, v
         after_hi2 = tile([P, 2 * I], BF16, "after_hi2", on="hi_win2")
         vv1, w_bf = after_hi2[:, 0:I], after_hi2[:, I : 2 * I]
         scale_out(bank1, fac[:, 0:4], vv1)
-        nc.vector.tensor_copy(lo_g[3][:, 0:n], lo_win[3][:].indirect(cls_list[:, 0 : n // 16]))
         scale_out(w_ps, fac[:, 4:8], w_bf)
-        vv01_w = tile([P, 2 * P], U32, "vv01_w", on="lo_win3")
+        raise_block(3, raised[3][:])
+        vv01_w = tile([P, 2 * P], U32, "vv01_w", on="val_win3")
         quantise(vv0[:], vv01_w[:, 0:P], vv_s[:, 0:P])
         quantise(vv1, vv01_w[:, P : 2 * P], vv_s[:, P : 2 * P])
-        raise_block(3, raised[3][:])
-        w_w = tile([P, Q], U32, "w_w", on="val_win3")
-        quantise(w_bf, w_w[:], w_s[:])
         bank3 = cap_block(3, raised[3][:], bounded[3][:], pieces=2)
         vv2 = tile([P, I], BF16, "vv2", on="hi_win3")
         vv3 = tile([P, I], BF16, "vv3")
         vv23_w = tile([P, 2 * P], U32, "vv23_w")
         scale_out(bank2, fac[:, 0:4], vv2[:])
+        w_w = tile([P, Q], U32, "w_w", on="hi_g3")
+        quantise(w_bf, w_w[:], w_s[:])
+        res = tile([P, E], F32, "res")
+        acc01 = ps.tile([P, 2 * P], F32, name="acc01", tag="turn1")
+        multiply(acc01[:], vv01_w[:], vv_s[:, 0 : 2 * P])
+        nc.scalar.copy(res[:, 0 : 2 * P], acc01[:])
+        nc.sync.dma_start(out[:, 0 : 2 * P], res[:, 0 : 2 * P])
         quantise(vv2[:], vv23_w[:, 0:P], vv_s[:, 2 * P : 3 * P])
         scale_out(bank3, fac[:, 0:4], vv3[:])
-        acc012 = ps.tile([P, 3 * P], F32, name="acc012", tag="turn2")
-        multiply(acc012[:, 0 : 2 * P], vv01_w[:], vv_s[:, 0 : 2 * P])
-        multiply(acc012[:, 2 * P : 3 * P], vv23_w[:, 0:P], vv_s[:, 2 * P : 3 * P])
-        store(0, acc012[:])
+        acc2 = ps.tile([P, P], F32, name="acc2", tag="turn2")
+        multiply(acc2[:], vv23_w[:, 0:P], vv_s[:, 2 * P : 3 * P])
+        nc.scalar.copy(res[:, 2 * P : 3 * P], acc2[:])
         quantise(vv3[:], vv23_w[:, P : 2 * P], vv_s[:, 3 * P : 4 * P])
         acc3 = ps.tile([P, P], F32, name="acc3", tag="w_ps")
         multiply(acc3[:], vv23_w[:, P : 2 * P], vv_s[:, 3 * P : 4 * P])
-        store(3 * P, acc3[:])
+        nc.scalar.copy(res[:, 3 * P : 4 * P], acc3[:])
+        nc.sync.dma_start(out[:, 2 * P : 4 * P], res[:, 2 * P : 4 * P])

from contextlib import ExitStack

import concourse.mybir as mybir
from concourse.masks import make_identity

F32 = mybir.dt.float32
BF16 = mybir.dt.bfloat16
I32 = mybir.dt.int32
U32 = mybir.dt.uint32
U16 = mybir.dt.uint16
U8 = mybir.dt.uint8
FP8X4 = mybir.dt.float8_e4m3fn_x4
ALU = mybir.AluOpType
ACT = mybir.ActivationFunctionType

P = 128
D, T, I, Q, E, U = 512, 1024, 512, 128, 512, 256
FLOPS = 2 * D * Q * I + 2 * I * Q * E
BLOCKS = E // P
BOUND_W = I + 16
LO3_ON_VECTOR = 256


def tile_attend_boundedvalues_kernel(tc, query, keys_words, keys_scales, size, vals, low, high, vsc, offs, offs2, out):
    nc = tc.nc
    with ExitStack() as ctx:
        sb = ctx.enter_context(tc.tile_pool(name="sb", bufs=1))
        ps = ctx.enter_context(tc.psum_pool(name="ps", bufs=1))

        def dealt(ap):
            return ap.rearrange("p (t b r) -> p b t r", t=4, r=8)

        def natural(ap):
            return ap.rearrange("p (b t r) -> p b t r", t=4, r=8)

        def tile(shape, dtype, name, on=None):
            return sb.tile(shape, dtype, name=name, tag=on or name, align_bytes=64)

        tok_list = sb.tile([P, I // 16], U16, name="tok_list")
        cls_list = sb.tile([P, I // 16], U16, name="cls_list")
        lo_win = [tile([P, BOUND_W], F32, f"lo_win{j}") for j in range(BLOCKS)]
        hi_win = [tile([P, BOUND_W], F32, f"hi_win{j}") for j in range(BLOCKS)]
        val_win = [tile([P, T], F32, f"val_win{j}") for j in range(BLOCKS)]
        q_raw = tile([P, 4, Q], F32, "q_raw")
        kw_win = tile([P, T], I32, "kw_win")
        ks_win = tile([P, T], U8, "ks_win")
        fac_rows = tile([P, P], F32, "fac_rows")
        ident = tile([P, P], F32, "ident")

        nc.vector.memset(ks_win[:].bitcast(I32), 0)
        nc.gpsimd.memset(fac_rows[:], 0.0)
        make_identity(nc, ident[:])
        for j in range(BLOCKS):
            eng = nc.vector if j < 2 else nc.gpsimd
            eng.memset(lo_win[j][:, U:], 0.0)
            eng.memset(hi_win[j][:, U:], 0.0)

        def load_lo(j):
            nc.sync.dma_start(lo_win[j][:, 0:U], low[j * P : (j + 1) * P, :])

        def load_hi(j):
            nc.sync.dma_start(hi_win[j][:, 0:U], high[j * P : (j + 1) * P, :])

        def load_val(j):
            nc.sync.dma_start(val_win[j][:], vals[j * P : (j + 1) * P, :])

        nc.sync.dma_start(cls_list[:], offs2)
        load_lo(0)
        nc.sync.dma_start(q_raw[:], query.rearrange("(p j) q -> p j q", j=4))
        load_hi(0)
        load_lo(1)
        load_hi(1)
        nc.sync.dma_start(tok_list[:], offs)
        nc.sync.dma_start(kw_win[:], keys_words[0].rearrange("p n t -> p (n t)").bitcast(I32))
        load_lo(3)
        load_val(0)
        for g in range(4):
            nc.sync.dma_start(ks_win[32 * g : 32 * g + 4, :].bitcast(I32), keys_scales[0, 4 * g : 4 * g + 4, :].bitcast(I32))
        load_val(1)
        load_lo(2)
        nc.sync.dma_start(fac_rows[0:4, :].rearrange("t (b r) -> t b r", r=8), vsc[:, 0].rearrange("(b t r) -> t b r", t=4, r=8))
        nc.sync.dma_start(fac_rows[4:8, :].rearrange("t (b r) -> t b r", r=8), size[0, :].rearrange("(b t r) -> t b r", t=4, r=8))
        load_val(2)
        load_hi(2)
        load_val(3)
        load_hi(3)

        lo_g = [tile([P, I], F32, f"lo_g{j}") for j in range(BLOCKS)]
        hi_g = [tile([P, I], F32, f"hi_g{j}") for j in range(BLOCKS)]
        val_g = [tile([P, I], F32, f"val_g{j}") for j in range(BLOCKS)]

        def gather_lo(j):
            nc.scalar.activation(lo_g[j][:], lo_win[j][:].indirect(cls_list[:]), ACT.Copy)

        def gather_hi(j):
            nc.scalar.activation(hi_g[j][:], hi_win[j][:].indirect(cls_list[:]), ACT.Copy)

        def gather_val(j):
            nc.scalar.activation(val_g[j][:], val_win[j][:].indirect(tok_list[:]), ACT.Copy)

        def turn(src, bank):
            for t in range(4):
                nc.tensor.transpose(bank[:, t, :], src[:, t * P : (t + 1) * P], ident[:])

        def scale_out(bank, factor, dst):
            nc.vector.tensor_tensor(dst.rearrange("p (c t) -> p c t", t=4), bank[:].rearrange("p t c -> p c t"), factor.unsqueeze(1).to_broadcast([P, P, 4]), ALU.mult)

        def quantise(src, words, scales):
            nc.vector.quantize_mx(out=words.bitcast(FP8X4), scales=scales, in_=src)

        def raise_block(j, raised):
            nc.vector.tensor_tensor(raised, val_g[j][:], lo_g[j][:], ALU.max)

        def cap_block(j, raised, bounded, pieces=1):
            bank = ps.tile([P, 4, P], F32, name=f"turned{j}", tag=f"turn{j % 3}")
            n = 4 // pieces
            for t0 in range(0, 4, n):
                ts = slice(t0, t0 + n)
                nc.vector.tensor_tensor(dealt(bounded)[:, :, ts, :], natural(raised)[:, :, ts, :], natural(hi_g[j][:])[:, :, ts, :], ALU.min)
            turn(bounded, bank)
            return bank

        def multiply(acc, words, scales):
            nc.tensor.matmul_mx(out=acc, lhsT=w_w[:].bitcast(FP8X4), lhsT_scale=w_s[:], rhs=words.bitcast(FP8X4), rhs_scale=scales, start=True, stop=True)

        kw_g = tile([P, I], U32, "kw_g")
        ks_g = tile([P, I], U8, "ks_g")
        q_bf = tile([P, 4 * Q], BF16, "q_bf")
        q_w = tile([P, Q], U32, "q_w")
        q_s = tile([P, Q], U8, "q_s")
        row_sum = tile([P, 1], F32, "row_sum")
        inv_sum = tile([P, 1], F32, "inv_sum")
        p_norm = tile([P, I], F32, "p_norm")
        w_s = tile([P, Q], U8, "w_s")
        fac = tile([P, 8], F32, "fac")
        vv_s = tile([P, E], U8, "vv_s")

        def gather_halves_on_vector(dst, win):
            for h in range(2):
                nc.vector.tensor_copy(dst[:, h * 256 : (h + 1) * 256], win[:].indirect(cls_list[:, h * 16 : (h + 1) * 16]))

        gather_halves_on_vector(lo_g[0], lo_win[0])
        nc.scalar.activation(q_bf[:].rearrange("p (q j) -> p q j", j=4), q_raw[:].rearrange("p j q -> p q j"), ACT.Copy)
        gather_halves_on_vector(hi_g[0], hi_win[0])
        gather_lo(1)
        gather_hi(1)
        n = LO3_ON_VECTOR
        nc.scalar.activation(lo_g[3][:, n:I], lo_win[3][:].indirect(cls_list[:, n // 16 : I // 16]), ACT.Copy)
        gather_val(0)
        quantise(q_bf[:], q_w[:], q_s[:])
        nc.vector.tensor_copy(kw_g[:], kw_win[:].bitcast(U32).indirect(tok_list[:]))
        nc.vector.tensor_copy(lo_g[3][:, 0:n], lo_win[3][:].indirect(cls_list[:, 0 : n // 16]))
        nc.vector.tensor_copy(ks_g[:], ks_win[:].indirect(tok_list[:]))
        scores = ps.tile([P, I], F32, name="scores", tag="scores")
        nc.tensor.matmul_mx(out=scores[:], lhsT=q_w[:].bitcast(FP8X4), lhsT_scale=q_s[:], rhs=kw_g[:].bitcast(FP8X4), rhs_scale=ks_g[:], start=True, stop=True)
        raised = [tile([P, I], F32, f"raised{j}", on="ks_win" if j == 0 else None) for j in range(BLOCKS)]
        raise_block(0, raised[0][:])
        neg_max = tile([P, 1], F32, "neg_max")
        nc.vector.tensor_reduce(neg_max[:], scores[:], mybir.AxisListType.X, ALU.max, negate=True)
        gather_val(1)
        gather_lo(2)
        p_exp = tile([P, I], F32, "p_exp", on="lo_win2")
        nc.scalar.activation(dealt(p_exp[:]), natural(scores[:]), ACT.Exp, bias=neg_max[:], accum_out=row_sum[:])
        gather_val(2)
        gather_hi(2)
        gather_val(3)
        gather_hi(3)

        bounded = [tile([P, I], F32, f"bounded{j}", on="val_win1" if j == 0 else None) for j in range(BLOCKS)]
        fac_ps = ps.tile([P, P], F32, name="fac_ps", tag="fac_ps")
        nc.tensor.transpose(fac_ps[:], fac_rows[:], ident[:])
        raise_block(1, raised[1][:])
        bank0 = cap_block(0, raised[0][:], bounded[0][:])
        bank1 = cap_block(1, raised[1][:], bounded[1][:])
        nc.vector.reciprocal(inv_sum[:], row_sum[:])
        nc.vector.tensor_copy(fac[:], fac_ps[:, 0:8])
        nc.vector.tensor_scalar(p_norm[:], p_exp[:], inv_sum[:], None, ALU.mult)
        w_ps = ps.tile([P, 4, Q], F32, name="w_ps", tag="w_ps")
        turn(p_norm, w_ps)
        raise_block(2, raised[2][:])
        vv0 = tile([P, I], BF16, "vv0", on="val_win2")
        scale_out(bank0, fac[:, 0:4], vv0[:])
        bank2 = cap_block(2, raised[2][:], bounded[2][:])
        after_hi2 = tile([P, 2 * I], BF16, "after_hi2", on="hi_win2")
        vv1, w_bf = after_hi2[:, 0:I], after_hi2[:, I : 2 * I]
        scale_out(bank1, fac[:, 0:4], vv1)
        scale_out(w_ps, fac[:, 4:8], w_bf)
        raise_block(3, raised[3][:])
        vv01_w = tile([P, 2 * P], U32, "vv01_w", on="val_win3")
        quantise(vv0[:], vv01_w[:, 0:P], vv_s[:, 0:P])
        quantise(vv1, vv01_w[:, P : 2 * P], vv_s[:, P : 2 * P])
        bank3 = cap_block(3, raised[3][:], bounded[3][:], pieces=2)
        vv2 = tile([P, I], BF16, "vv2", on="hi_win3")
        vv3 = tile([P, I], BF16, "vv3")
        vv23_w = tile([P, 2 * P], U32, "vv23_w")
        scale_out(bank2, fac[:, 0:4], vv2[:])
        w_w = tile([P, Q], U32, "w_w", on="hi_g3")
        quantise(w_bf, w_w[:], w_s[:])
        res = tile([P, E], F32, "res")
        acc01 = ps.tile([P, 2 * P], F32, name="acc01", tag="turn1")
        multiply(acc01[:], vv01_w[:], vv_s[:, 0 : 2 * P])
        nc.scalar.copy(res[:, 0 : 2 * P], acc01[:])
        nc.sync.dma_start(out[:, 0 : 2 * P], res[:, 0 : 2 * P])
        quantise(vv2[:], vv23_w[:, 0:P], vv_s[:, 2 * P : 3 * P])
        scale_out(bank3, fac[:, 0:4], vv3[:])
        acc2 = ps.tile([P, P], F32, name="acc2", tag="turn2")
        multiply(acc2[:], vv23_w[:, 0:P], vv_s[:, 2 * P : 3 * P])
        nc.scalar.copy(res[:, 2 * P : 3 * P], acc2[:])
        quantise(vv3[:], vv23_w[:, P : 2 * P], vv_s[:, 3 * P : 4 * P])
        acc3 = ps.tile([P, P], F32, name="acc3", tag="w_ps")
        multiply(acc3[:], vv23_w[:, P : 2 * P], vv_s[:, 3 * P : 4 * P])
        nc.scalar.copy(res[:, 3 * P : 4 * P], acc3[:])
        nc.sync.dma_start(out[:, 2 * P : 4 * P], res[:, 2 * P : 4 * P])
